import numpy as np, ml_dtypes
CORES = [8,11,14,16,19,22,24,27,30]
N = 9
TK = 64
def setup_inputs(rng):
    rt = (0.75 * rng.standard_normal((128, 1), dtype=np.float32) + rng.standard_normal((128, N), dtype=np.float32) / 2).astype(ml_dtypes.bfloat16)
    return {"x": rng.standard_normal((N, 128, TK), dtype=np.float32).astype(ml_dtypes.bfloat16), "rt": np.broadcast_to(rt, (N, 128, N)).copy(), "w": rng.standard_normal((N, 128, 128), dtype=np.float32).astype(ml_dtypes.bfloat16)}
def setup_inputs_big(rng):
    d = setup_inputs(rng)
    for k in ("x", "w"): d[k] = (d[k].astype(np.float32) * 1024.0).astype(d[k].dtype)
    return d
def setup_inputs_small(rng):
    d = setup_inputs(rng)
    for k in ("x", "w"): d[k] = (d[k].astype(np.float32) * (1 / 1024.0)).astype(d[k].dtype)
    return d
def reference(x, rt, w):
    X, RT, W = x.astype(np.float64), rt.astype(np.float64), w.astype(np.float64)
    y = np.zeros((N, 128, TK))
    for r in range(N):
        sc = RT[r].T @ X[r]
        g = np.exp(sc - sc.max(axis=0)); g = g / g.sum(axis=0)
        y[r] = sum(g[j] * (W[j].T @ X[r]) for j in range(N))
    return {"y": y.astype(ml_dtypes.bfloat16)}

@@ -1,0 +1,213 @@
+from concourse.bass import DstId, RemoteDMATransfer
+from concourse.mybir import AluOpType, AxisListType, ActivationFunctionType
+
+N = 9
+D = 128
+TK = 64
+NA = 5
+
+SCRATCH = {
+    "wall": ("sbuf", [128, N * D], "bfloat16"),
+    "xs": ("sbuf", [128, TK], "bfloat16"),
+    "rts": ("sbuf", [128, N], "bfloat16"),
+    "ident": ("sbuf", [128, 128], "bfloat16"),
+    "xt": ("sbuf", [128, D], "bfloat16"),
+    "nm": ("sbuf", [128, 4], "float32"),
+    "ex": ("sbuf", [128, 12], "float32"),
+    "ssum": ("sbuf", [128, 4], "float32"),
+    "rs": ("sbuf", [128, 4], "float32"),
+    "dg": ("sbuf", [128, N * TK], "bfloat16"),
+    "xg": ("sbuf", [128, N * TK], "bfloat16"),
+    "ysb": ("sbuf", [128, TK], "bfloat16"),
+    "ps_s": ("psum", [128, 512], "float32"),
+    "ps_t": ("psum", [128, 512], "float32"),
+    "ps_a": ("psum", [128, 512], "float32"),
+    "ps_b": ("psum", [128, 512], "float32"),
+    "ps_y": ("psum", [128, 512], "float32"),
+}
+SEMAPHORES = (["ldw", "ldx", "ms", "idn", "p_s", "p_t", "p_a", "p_b", "p_y", "v_nm", "v_xt", "v_rs", "v_da", "v_db",
+               "a_e", "c_a", "c_b", "v_y", "st", "loc"]
+              + ["h%d" % i for i in range(N)]
+              + ["r%d" % i for i in range(N)]
+              + ["f%d" % i for i in range(N)])
+
+
+def _engines(mask):
+    return [e for e in range(mask.bit_length()) if (mask >> e) & 1]
+
+
+def _mask(engines):
+    return sum(1 << e for e in engines)
+
+
+def make_plan(cores, topo):
+    chips = sorted(set(topo.chip(c) for c in cores))
+    mem = {ch: [c for c in cores if topo.chip(c) == ch] for ch in chips}
+
+    def reach(s, ch):
+        return all(topo.may_write(s, d) for d in mem[ch])
+
+    load = {c: 0 for c in cores}
+    relays = []
+    for a in chips:
+        for s in mem[a]:
+            for b in chips:
+                if b == a or reach(s, b):
+                    continue
+                cands = [p for p in mem[a] if p != s and reach(p, b)]
+                p = min(cands, key=lambda q: (load[q], sum(topo.die(z) == topo.die(q) for z in mem[a])))
+                load[p] += len(mem[b])
+                relays.append((s, p, b))
+    collect = {c: [] for c in cores}
+    collector = {}
+    for b in chips:
+        groups = [[s for s in mem[a] if reach(s, b)] for a in chips if a != b]
+        for grp in sorted(groups, key=lambda x: -len(x)):
+            p = min(mem[b], key=lambda q: load[q])
+            if not collect[p]:
+                load[p] += 1
+            collect[p] += grp
+            for s in grp:
+                collector[(s, b)] = p
+    slot = {}
+    for b in chips:
+        order = list(mem[b])
+        for p in mem[b]:
+            order += collect[p]
+        order += [s for (s, p, bb) in relays if bb == b]
+        slot[b] = {s: i for i, s in enumerate(order)}
+    return {"chips": chips, "mem": mem, "relays": relays, "collect": collect, "collector": collector, "slot": slot}
+
+
+def rank_program(g, core, T, topo):
+    rank = T.rank_of(core)
+    if rank is None:
+        return
+    cores = list(T.cores)
+    rk = {c: i for i, c in enumerate(cores)}
+    plan = make_plan(cores, topo)
+    S = T.sem
+    pe, ve, ac, sp = g.tensor, g.vector, g.scalar, g.sync
+    mult = AluOpType.mult
+
+    def blocks(ch, first, n=1):
+        k = plan["slot"][ch][first]
+        return T.wall[:, k * D:(k + n) * D]
+
+    def dst_id(c):
+        rid, pid, _ = topo.addr(c)
+        return DstId(rid=rid, pnc=pid)
+
+    def first_write(c):
+        ch = topo.chip(c)
+        peers = [p for p in plan["mem"][ch] if p != c]
+        relaying = [p for (s, p, b) in plan["relays"] if s == c]
+        peers.sort(key=lambda p: p not in relaying)
+        away = [plan["collector"][(c, b)] for b in plan["chips"] if (c, b) in plan["collector"]]
+        on = _engines(topo.mask(c, peers[0]))
+        if not away:
+            return [(peers, on)]
+        off = _engines(topo.mask(c, away[0]))
+        out = [(peers, [e for e in on if e not in off])]
+        share = len(off) // len(away)
+        return out + [([d], off[i * share:(i + 1) * share]) for i, d in enumerate(away)]
+
+    def h_count(s, c):
+        return sum(len(eng) for (dsts, eng) in first_write(s) if c in dsts)
+
+    me = topo.chip(core)
+    peers = [p for p in plan["mem"][me] if p != core]
+
+    sp.dma_start(blocks(me, core), T.w[:, :]).then_inc(S.ldw, 16)
+    ac.dma_start(T.xs[:, :], T.x[:, :]).then_inc(S.ldx, 16)
+    sp.dma_start(T.rts[:, :], T.rt[:, :]).then_inc(S.ldx, 16)
+
+    ve.memset(T.ident[:, :], 1.0).then_inc(S.ms, 1)
+    g.wait_ge(S.ms, 1)
+    g.affine_select(T.ident[:, :], T.ident[:, :], [[-1, 128]], AluOpType.is_equal, 0.0, 0, 1).then_inc(S.idn, 1)
+
+    sent = 0
+    g.wait_ge(S.ldw, 16)
+    trs = []
+    for dsts, eng in first_write(core):
+        trs.append(RemoteDMATransfer(dst_ids=[dst_id(d) for d in dsts], dma_engine_mask=_mask(eng),
+                                     remote_sem=S["h%d" % rank], srcs=[blocks(me, core)],
+                                     dsts=[blocks(topo.chip(d), core) for d in dsts]))
+        sent += len(eng)
+    g.remote_dma_fused(trs, local_sem=S.loc)
+    for (s, p, b) in plan["relays"]:
+        if p != core:
+            continue
+        dsts = plan["mem"][b]
+        eng = _engines(topo.mask(core, dsts[0]))
+        g.wait_ge(S["h%d" % rk[s]], h_count(s, core))
+        g.remote_dma_fused([RemoteDMATransfer(dst_ids=[dst_id(d) for d in dsts], dma_engine_mask=_mask(eng),
+                                              remote_sem=S["r%d" % rk[s]], srcs=[blocks(me, s)],
+                                              dsts=[blocks(b, s) for d in dsts])], local_sem=S.loc)
+        sent += len(eng)
+    mine = plan["collect"][core]
+    if mine:
+        eng = _engines(topo.mask(core, peers[0]))
+        for s in mine:
+            g.wait_ge(S["h%d" % rk[s]], h_count(s, core))
+        g.remote_dma_fused([RemoteDMATransfer(dst_ids=[dst_id(d) for d in peers], dma_engine_mask=_mask(eng),
+                                              remote_sem=S["f%d" % rank], srcs=[blocks(me, mine[0], len(mine))],
+                                              dsts=[blocks(me, mine[0], len(mine)) for d in peers])],
+                           local_sem=S.loc)
+        sent += len(eng)
+    g.wait_ge(S.loc, sent)
+
+    h = slice(0, TK)
+    pe.wait_ge(S.ldx, 32)
+    pe.matmul(T.ps_s[h, 0:N], T.xs[:, :], T.rts[:, :], True, True).then_inc(S.p_s, 1)
+    pe.wait_ge(S.idn, 1)
+    pe.matmul(T.ps_t[h, 0:D], T.xs[:, :], T.ident[:, :], True, True).then_inc(S.p_t, 1)
+
+    ve.wait_ge(S.p_s, 1)
+    ve.tensor_reduce(T.nm[h, 0:1], T.ps_s[h, 0:N], AxisListType.X, AluOpType.max, negate=True).then_inc(S.v_nm, 1)
+    ac.wait_ge(S.v_nm, 1)
+    ac.activation(T.ex[h, 0:N], T.ps_s[h, 0:N], ActivationFunctionType.Exp, bias=T.nm[h, 0:1], scale=1.0,
+                  accum_out=T.ssum[h, 0:1]).then_inc(S.a_e, 1)
+    ve.wait_ge(S.p_t, 1)
+    ve.tensor_copy(T.xt[h, :], T.ps_t[h, 0:D]).then_inc(S.v_xt, 1)
+    ve.wait_ge(S.a_e, 1)
+    ve.reciprocal(T.rs[h, 0:1], T.ssum[h, 0:1]).then_inc(S.v_rs, 1)
+    ve.wait_ge(S.v_rs, 1)
+    ve.wait_ge(S.idn, 1)
+    for j in range(N):
+        ve.tensor_scalar(T.dg[h, j * TK:(j + 1) * TK], T.ident[h, 0:TK], T.ex[h, j:j + 1], T.rs[h, 0:1],
+                         mult, mult).then_inc(S.v_da if j < NA else S.v_db, 1)
+    pe.wait_ge(S.v_xt, 1)
+    pe.wait_ge(S.v_da, NA)
+    pe.matmul(T.ps_a[:, 0:NA * TK], T.xt[h, :], T.dg[h, 0:NA * TK], True, True).then_inc(S.p_a, 1)
+    pe.wait_ge(S.v_db, N - NA)
+    pe.matmul(T.ps_b[:, 0:(N - NA) * TK], T.xt[h, :], T.dg[h, NA * TK:N * TK], True, True).then_inc(S.p_b, 1)
+    ve.wait_ge(S.p_a, 1)
+    ve.tensor_copy(T.xg[:, 0:NA * TK], T.ps_a[:, 0:NA * TK]).then_inc(S.c_a, 1)
+    ac.wait_ge(S.p_b, 1)
+    ac.activation(T.xg[:, NA * TK:N * TK], T.ps_b[:, 0:(N - NA) * TK], ActivationFunctionType.Copy).then_inc(S.c_b, 1)
+
+    arrivals = [(S.ldw, 16, [core])]
+    arrivals += [(S["h%d" % rk[s]], h_count(s, core), [s]) for s in peers + mine]
+    for p in peers:
+        if plan["collect"][p]:
+            arrivals.append((S["f%d" % rk[p]], len(_engines(topo.mask(p, core))), plan["collect"][p]))
+    for (s, p, b) in plan["relays"]:
+        if b == me:
+            arrivals.append((S["r%d" % rk[s]], len(_engines(topo.mask(p, core))), [s]))
+    pe.wait_ge(S.c_a, 1)
+    pe.wait_ge(S.c_b, 1)
+    done = 0
+    for sem, count, owners in arrivals:
+        pe.wait_ge(sem, count)
+        for s in owners:
+            j = rk[s]
+            done += 1
+            mm = pe.matmul(T.ps_y[:, 0:TK], blocks(me, s), T.xg[:, j * TK:(j + 1) * TK], done == 1, done == N)
+    mm.then_inc(S.p_y, 1)
+
+    ve.wait_ge(S.p_y, 1)
+    ve.tensor_copy(T.ysb[:, :], T.ps_y[:, 0:TK]).then_inc(S.v_y, 1)
+    sp.wait_ge(S.v_y, 1)
+    sp.dma_start(T.y[:, :], T.ysb[:, :]).then_inc(S.st, 16)
+    sp.wait_ge(S.st, 16)

@@ -8,6 +8,8 @@ NA = 5
 
 SCRATCH = {
     "wall": ("sbuf", [128, N * D], "bfloat16"),
+    "wd": ("dram", [128, D], "bfloat16"),
+    "rd": ("dram", [128, D], "bfloat16"),
     "xs": ("sbuf", [128, TK], "bfloat16"),
     "rts": ("sbuf", [128, N], "bfloat16"),
     "ident": ("sbuf", [128, 128], "bfloat16"),
@@ -25,9 +27,10 @@ SCRATCH = {
     "ps_b": ("psum", [128, 512], "float32"),
     "ps_y": ("psum", [128, 512], "float32"),
 }
-SEMAPHORES = (["ldw", "ldx", "ms", "idn", "p_s", "p_t", "p_a", "p_b", "p_y", "v_nm", "v_xt", "v_rs", "v_da", "v_db",
-               "a_e", "c_a", "c_b", "v_y", "st", "loc"]
+SEMAPHORES = (["ldd", "ldw", "ldx", "ms", "idn", "p_s", "p_t", "p_a", "p_b", "p_y", "v_nm", "v_xt", "v_rs", "v_da",
+               "v_db", "a_e", "c_a", "c_b", "v_y", "st", "loc"]
               + ["h%d" % i for i in range(N)]
+              + ["q%d" % i for i in range(N)]
               + ["r%d" % i for i in range(N)]
               + ["f%d" % i for i in range(N)])
 
@@ -38,6 +41,15 @@ def _engines(mask):
 
 def _mask(engines):
     return sum(1 << e for e in engines)
+
+
+def free_engines(p, mem, relays, topo):
+    nb = [q for q in mem[topo.chip(p)] if q != p]
+    on = _engines(topo.mask(p, nb[0]))
+    for (s, q, b) in relays:
+        if q == p:
+            on = [e for e in on if e not in _engines(topo.mask(p, mem[b][0]))]
+    return on
 
 
 def make_plan(cores, topo):
@@ -61,14 +73,11 @@ def make_plan(cores, topo):
     collect = {c: [] for c in cores}
     collector = {}
     for b in chips:
-        groups = [[s for s in mem[a] if reach(s, b)] for a in chips if a != b]
-        for grp in sorted(groups, key=lambda x: -len(x)):
-            p = min(mem[b], key=lambda q: load[q])
-            if not collect[p]:
-                load[p] += 1
-            collect[p] += grp
-            for s in grp:
-                collector[(s, b)] = p
+        cap = {p: len(free_engines(p, mem, relays, topo)) for p in mem[b]}
+        for s in [s for a in chips if a != b for s in mem[a] if reach(s, b)]:
+            p = min(mem[b], key=lambda q: ((len(collect[q]) + 1) / cap[q], topo.die(q) != topo.die(s)))
+            collect[p].append(s)
+            collector[(s, b)] = p
     slot = {}
     for b in chips:
         order = list(mem[b])
@@ -98,64 +107,83 @@ def rank_program(g, core, T, topo):
         rid, pid, _ = topo.addr(c)
         return DstId(rid=rid, pnc=pid)
 
-    def first_write(c):
-        ch = topo.chip(c)
-        peers = [p for p in plan["mem"][ch] if p != c]
-        relaying = [p for (s, p, b) in plan["relays"] if s == c]
-        peers.sort(key=lambda p: p not in relaying)
-        away = [plan["collector"][(c, b)] for b in plan["chips"] if (c, b) in plan["collector"]]
-        on = _engines(topo.mask(c, peers[0]))
-        if not away:
-            return [(peers, on)]
-        off = _engines(topo.mask(c, away[0]))
-        out = [(peers, [e for e in on if e not in off])]
-        share = len(off) // len(away)
-        return out + [([d], off[i * share:(i + 1) * share]) for i, d in enumerate(away)]
+    def serve(c):
+        return free_engines(c, plan["mem"], plan["relays"], topo)
 
-    def h_count(s, c):
-        return sum(len(eng) for (dsts, eng) in first_write(s) if c in dsts)
+    def first_calls(c):
+        ch = topo.chip(c)
+        nb = [p for p in plan["mem"][ch] if p != c]
+        relaying = [p for (s, p, b) in plan["relays"] if s == c]
+        away = [plan["collector"][(c, b)] for b in plan["chips"] if (c, b) in plan["collector"]]
+        on = _engines(topo.mask(c, nb[0]))
+        per = len(on) // 2 // (len(away) + (1 if relaying else 0))
+        first = []
+        if away:
+            off = _engines(topo.mask(c, away[0]))
+            on = [e for e in on if e not in off]
+            off = off[::len(off) // (per * len(away))]
+            first = [("h", [d], off[i * per:(i + 1) * per]) for i, d in enumerate(away)]
+        if relaying:
+            first = [("q", relaying, on[::len(on) // per])] + first
+        return [first, [("h", nb, serve(c))]]
+
+    def count(kind, s, c):
+        return sum(len(eng) for call in first_calls(s) for (k, dsts, eng) in call if k == kind and c in dsts)
 
     me = topo.chip(core)
     peers = [p for p in plan["mem"][me] if p != core]
+    mine = plan["collect"][core]
 
-    sp.dma_start(blocks(me, core), T.w[:, :]).then_inc(S.ldw, 16)
+    sp.dma_start(T.wd[:, :], T.w[:, :]).then_inc(S.ldd, 16)
     ac.dma_start(T.xs[:, :], T.x[:, :]).then_inc(S.ldx, 16)
     sp.dma_start(T.rts[:, :], T.rt[:, :]).then_inc(S.ldx, 16)
+    ac.dma_start(blocks(me, core), T.w[:, :]).then_inc(S.ldw, 16)
 
     ve.memset(T.ident[:, :], 1.0).then_inc(S.ms, 1)
     g.wait_ge(S.ms, 1)
     g.affine_select(T.ident[:, :], T.ident[:, :], [[-1, 128]], AluOpType.is_equal, 0.0, 0, 1).then_inc(S.idn, 1)
 
     sent = 0
-    g.wait_ge(S.ldw, 16)
-    trs = []
-    for dsts, eng in first_write(core):
-        trs.append(RemoteDMATransfer(dst_ids=[dst_id(d) for d in dsts], dma_engine_mask=_mask(eng),
-                                     remote_sem=S["h%d" % rank], srcs=[blocks(me, core)],
-                                     dsts=[blocks(topo.chip(d), core) for d in dsts]))
-        sent += len(eng)
-    g.remote_dma_fused(trs, local_sem=S.loc)
+    g.wait_ge(S.ldd, 16)
+    for call in first_calls(core):
+        trs = []
+        for kind, dsts, eng in call:
+            trs.append(RemoteDMATransfer(dst_ids=[dst_id(d) for d in dsts], dma_engine_mask=_mask(eng),
+                                         remote_sem=S["%s%d" % (kind, rank)], srcs=[T.wd[:, :]],
+                                         dsts=[T.rd[:, :] if kind == "q" else blocks(topo.chip(d), core)
+                                               for d in dsts]))
+            sent += len(eng)
+        g.remote_dma_fused(trs, local_sem=S.loc)
     for (s, p, b) in plan["relays"]:
         if p != core:
             continue
         dsts = plan["mem"][b]
         eng = _engines(topo.mask(core, dsts[0]))
-        g.wait_ge(S["h%d" % rk[s]], h_count(s, core))
+        g.wait_ge(S["q%d" % rk[s]], count("q", s, core))
         g.remote_dma_fused([RemoteDMATransfer(dst_ids=[dst_id(d) for d in dsts], dma_engine_mask=_mask(eng),
-                                              remote_sem=S["r%d" % rk[s]], srcs=[blocks(me, s)],
+                                              remote_sem=S["r%d" % rk[s]], srcs=[T.rd[:, :]],
                                               dsts=[blocks(b, s) for d in dsts])], local_sem=S.loc)
         sent += len(eng)
-    mine = plan["collect"][core]
     if mine:
-        eng = _engines(topo.mask(core, peers[0]))
+        eng = serve(core)
         for s in mine:
-            g.wait_ge(S["h%d" % rk[s]], h_count(s, core))
+            g.wait_ge(S["h%d" % rk[s]], count("h", s, core))
         g.remote_dma_fused([RemoteDMATransfer(dst_ids=[dst_id(d) for d in peers], dma_engine_mask=_mask(eng),
                                               remote_sem=S["f%d" % rank], srcs=[blocks(me, mine[0], len(mine))],
                                               dsts=[blocks(me, mine[0], len(mine)) for d in peers])],
                            local_sem=S.loc)
         sent += len(eng)
     g.wait_ge(S.loc, sent)
+
+    arrivals = [(S.ldw, 16, [core])]
+    arrivals += [(S["h%d" % rk[s]], count("h", s, core), [s]) for s in peers + mine]
+    for p in peers:
+        if plan["collect"][p]:
+            arrivals.append((S["f%d" % rk[p]], len(serve(p)), plan["collect"][p]))
+    for (s, p, b) in plan["relays"]:
+        if b == me:
+            arrivals.append((S["r%d" % rk[s]], len(_engines(topo.mask(p, core))), [s]))
+    order = [s for (sem, cnt, owners) in arrivals for s in owners]
 
     h = slice(0, TK)
     pe.wait_ge(S.ldx, 32)
@@ -168,15 +196,22 @@ def rank_program(g, core, T, topo):
     ac.wait_ge(S.v_nm, 1)
     ac.activation(T.ex[h, 0:N], T.ps_s[h, 0:N], ActivationFunctionType.Exp, bias=T.nm[h, 0:1], scale=1.0,
                   accum_out=T.ssum[h, 0:1]).then_inc(S.a_e, 1)
-    ve.wait_ge(S.p_t, 1)
-    ve.tensor_copy(T.xt[h, :], T.ps_t[h, 0:D]).then_inc(S.v_xt, 1)
+    ac.wait_ge(S.a_e, 1)
+    ac.wait_ge(S.idn, 1)
+    for k in range(NA):
+        j = rk[order[k]]
+        ac.activation(T.dg[h, k * TK:(k + 1) * TK], T.ident[h, 0:TK], ActivationFunctionType.Copy,
+                      scale=T.ex[h, j:j + 1]).then_inc(S.v_da, 1)
     ve.wait_ge(S.a_e, 1)
     ve.reciprocal(T.rs[h, 0:1], T.ssum[h, 0:1]).then_inc(S.v_rs, 1)
     ve.wait_ge(S.v_rs, 1)
+    ve.wait_ge(S.p_t, 1)
+    ve.tensor_scalar(T.xt[h, :], T.ps_t[h, 0:D], T.rs[h, 0:1], None, mult).then_inc(S.v_xt, 1)
     ve.wait_ge(S.idn, 1)
-    for j in range(N):
-        ve.tensor_scalar(T.dg[h, j * TK:(j + 1) * TK], T.ident[h, 0:TK], T.ex[h, j:j + 1], T.rs[h, 0:1],
-                         mult, mult).then_inc(S.v_da if j < NA else S.v_db, 1)
+    for k in range(NA, N):
+        j = rk[order[k]]
+        ve.tensor_scalar(T.dg[h, k * TK:(k + 1) * TK], T.ident[h, 0:TK], T.ex[h, j:j + 1], None,
+                         mult).then_inc(S.v_db, 1)
     pe.wait_ge(S.v_xt, 1)
     pe.wait_ge(S.v_da, NA)
     pe.matmul(T.ps_a[:, 0:NA * TK], T.xt[h, :], T.dg[h, 0:NA * TK], True, True).then_inc(S.p_a, 1)
@@ -187,23 +222,15 @@ def rank_program(g, core, T, topo):
     ac.wait_ge(S.p_b, 1)
     ac.activation(T.xg[:, NA * TK:N * TK], T.ps_b[:, 0:(N - NA) * TK], ActivationFunctionType.Copy).then_inc(S.c_b, 1)
 
-    arrivals = [(S.ldw, 16, [core])]
-    arrivals += [(S["h%d" % rk[s]], h_count(s, core), [s]) for s in peers + mine]
-    for p in peers:
-        if plan["collect"][p]:
-            arrivals.append((S["f%d" % rk[p]], len(_engines(topo.mask(p, core))), plan["collect"][p]))
-    for (s, p, b) in plan["relays"]:
-        if b == me:
-            arrivals.append((S["r%d" % rk[s]], len(_engines(topo.mask(p, core))), [s]))
+    k = 0
     pe.wait_ge(S.c_a, 1)
-    pe.wait_ge(S.c_b, 1)
-    done = 0
-    for sem, count, owners in arrivals:
-        pe.wait_ge(sem, count)
+    for sem, cnt, owners in arrivals:
+        pe.wait_ge(sem, cnt)
         for s in owners:
-            j = rk[s]
-            done += 1
-            mm = pe.matmul(T.ps_y[:, 0:TK], blocks(me, s), T.xg[:, j * TK:(j + 1) * TK], done == 1, done == N)
+            if k == NA:
+                pe.wait_ge(S.c_b, 1)
+            mm = pe.matmul(T.ps_y[:, 0:TK], blocks(me, s), T.xg[:, k * TK:(k + 1) * TK], k == 0, k == N - 1)
+            k += 1
     mm.then_inc(S.p_y, 1)
 
     ve.wait_ge(S.p_y, 1)

from concourse.bass import DstId, RemoteDMATransfer
from concourse.mybir import AluOpType, AxisListType, ActivationFunctionType

N = 9
D = 128
TK = 64
NA = 5

SCRATCH = {
    "wall": ("sbuf", [128, N * D], "bfloat16"),
    "wd": ("dram", [128, D], "bfloat16"),
    "rd": ("dram", [128, D], "bfloat16"),
    "xs": ("sbuf", [128, TK], "bfloat16"),
    "rts": ("sbuf", [128, N], "bfloat16"),
    "ident": ("sbuf", [128, 128], "bfloat16"),
    "xt": ("sbuf", [128, D], "bfloat16"),
    "nm": ("sbuf", [128, 4], "float32"),
    "ex": ("sbuf", [128, 12], "float32"),
    "ssum": ("sbuf", [128, 4], "float32"),
    "rs": ("sbuf", [128, 4], "float32"),
    "dg": ("sbuf", [128, N * TK], "bfloat16"),
    "xg": ("sbuf", [128, N * TK], "bfloat16"),
    "ysb": ("sbuf", [128, TK], "bfloat16"),
    "ps_s": ("psum", [128, 512], "float32"),
    "ps_t": ("psum", [128, 512], "float32"),
    "ps_a": ("psum", [128, 512], "float32"),
    "ps_b": ("psum", [128, 512], "float32"),
    "ps_y": ("psum", [128, 512], "float32"),
}
SEMAPHORES = (["ldd", "ldw", "ldx", "ms", "idn", "p_s", "p_t", "p_a", "p_b", "p_y", "v_nm", "v_xt", "v_rs", "v_da",
               "v_db", "a_e", "c_a", "c_b", "v_y", "st", "loc"]
              + ["h%d" % i for i in range(N)]
              + ["q%d" % i for i in range(N)]
              + ["r%d" % i for i in range(N)]
              + ["f%d" % i for i in range(N)])


def _engines(mask):
    return [e for e in range(mask.bit_length()) if (mask >> e) & 1]


def _mask(engines):
    return sum(1 << e for e in engines)


def free_engines(p, mem, relays, topo):
    nb = [q for q in mem[topo.chip(p)] if q != p]
    on = _engines(topo.mask(p, nb[0]))
    for (s, q, b) in relays:
        if q == p:
            on = [e for e in on if e not in _engines(topo.mask(p, mem[b][0]))]
    return on


def make_plan(cores, topo):
    chips = sorted(set(topo.chip(c) for c in cores))
    mem = {ch: [c for c in cores if topo.chip(c) == ch] for ch in chips}

    def reach(s, ch):
        return all(topo.may_write(s, d) for d in mem[ch])

    load = {c: 0 for c in cores}
    relays = []
    for a in chips:
        for s in mem[a]:
            for b in chips:
                if b == a or reach(s, b):
                    continue
                cands = [p for p in mem[a] if p != s and reach(p, b)]
                p = min(cands, key=lambda q: (load[q], sum(topo.die(z) == topo.die(q) for z in mem[a])))
                load[p] += len(mem[b])
                relays.append((s, p, b))
    collect = {c: [] for c in cores}
    collector = {}
    for b in chips:
        cap = {p: len(free_engines(p, mem, relays, topo)) for p in mem[b]}
        for s in [s for a in chips if a != b for s in mem[a] if reach(s, b)]:
            p = min(mem[b], key=lambda q: ((len(collect[q]) + 1) / cap[q], topo.die(q) != topo.die(s)))
            collect[p].append(s)
            collector[(s, b)] = p
    slot = {}
    for b in chips:
        order = list(mem[b])
        for p in mem[b]:
            order += collect[p]
        order += [s for (s, p, bb) in relays if bb == b]
        slot[b] = {s: i for i, s in enumerate(order)}
    return {"chips": chips, "mem": mem, "relays": relays, "collect": collect, "collector": collector, "slot": slot}


def rank_program(g, core, T, topo):
    rank = T.rank_of(core)
    if rank is None:
        return
    cores = list(T.cores)
    rk = {c: i for i, c in enumerate(cores)}
    plan = make_plan(cores, topo)
    S = T.sem
    pe, ve, ac, sp = g.tensor, g.vector, g.scalar, g.sync
    mult = AluOpType.mult

    def blocks(ch, first, n=1):
        k = plan["slot"][ch][first]
        return T.wall[:, k * D:(k + n) * D]

    def dst_id(c):
        rid, pid, _ = topo.addr(c)
        return DstId(rid=rid, pnc=pid)

    def serve(c):
        return free_engines(c, plan["mem"], plan["relays"], topo)

    def first_calls(c):
        ch = topo.chip(c)
        nb = [p for p in plan["mem"][ch] if p != c]
        relaying = [p for (s, p, b) in plan["relays"] if s == c]
        away = [plan["collector"][(c, b)] for b in plan["chips"] if (c, b) in plan["collector"]]
        on = _engines(topo.mask(c, nb[0]))
        per = len(on) // 2 // (len(away) + (1 if relaying else 0))
        first = []
        if away:
            off = _engines(topo.mask(c, away[0]))
            on = [e for e in on if e not in off]
            off = off[::len(off) // (per * len(away))]
            first = [("h", [d], off[i * per:(i + 1) * per]) for i, d in enumerate(away)]
        if relaying:
            first = [("q", relaying, on[::len(on) // per])] + first
        return [first, [("h", nb, serve(c))]]

    def count(kind, s, c):
        return sum(len(eng) for call in first_calls(s) for (k, dsts, eng) in call if k == kind and c in dsts)

    me = topo.chip(core)
    peers = [p for p in plan["mem"][me] if p != core]
    mine = plan["collect"][core]

    sp.dma_start(T.wd[:, :], T.w[:, :]).then_inc(S.ldd, 16)
    ac.dma_start(T.xs[:, :], T.x[:, :]).then_inc(S.ldx, 16)
    sp.dma_start(T.rts[:, :], T.rt[:, :]).then_inc(S.ldx, 16)
    ac.dma_start(blocks(me, core), T.w[:, :]).then_inc(S.ldw, 16)

    ve.memset(T.ident[:, :], 1.0).then_inc(S.ms, 1)
    g.wait_ge(S.ms, 1)
    g.affine_select(T.ident[:, :], T.ident[:, :], [[-1, 128]], AluOpType.is_equal, 0.0, 0, 1).then_inc(S.idn, 1)

    sent = 0
    g.wait_ge(S.ldd, 16)
    for call in first_calls(core):
        trs = []
        for kind, dsts, eng in call:
            trs.append(RemoteDMATransfer(dst_ids=[dst_id(d) for d in dsts], dma_engine_mask=_mask(eng),
                                         remote_sem=S["%s%d" % (kind, rank)], srcs=[T.wd[:, :]],
                                         dsts=[T.rd[:, :] if kind == "q" else blocks(topo.chip(d), core)
                                               for d in dsts]))
            sent += len(eng)
        g.remote_dma_fused(trs, local_sem=S.loc)
    for (s, p, b) in plan["relays"]:
        if p != core:
            continue
        dsts = plan["mem"][b]
        eng = _engines(topo.mask(core, dsts[0]))
        g.wait_ge(S["q%d" % rk[s]], count("q", s, core))
        g.remote_dma_fused([RemoteDMATransfer(dst_ids=[dst_id(d) for d in dsts], dma_engine_mask=_mask(eng),
                                              remote_sem=S["r%d" % rk[s]], srcs=[T.rd[:, :]],
                                              dsts=[blocks(b, s) for d in dsts])], local_sem=S.loc)
        sent += len(eng)
    if mine:
        eng = serve(core)
        for s in mine:
            g.wait_ge(S["h%d" % rk[s]], count("h", s, core))
        g.remote_dma_fused([RemoteDMATransfer(dst_ids=[dst_id(d) for d in peers], dma_engine_mask=_mask(eng),
                                              remote_sem=S["f%d" % rank], srcs=[blocks(me, mine[0], len(mine))],
                                              dsts=[blocks(me, mine[0], len(mine)) for d in peers])],
                           local_sem=S.loc)
        sent += len(eng)
    g.wait_ge(S.loc, sent)

    arrivals = [(S.ldw, 16, [core])]
    arrivals += [(S["h%d" % rk[s]], count("h", s, core), [s]) for s in peers + mine]
    for p in peers:
        if plan["collect"][p]:
            arrivals.append((S["f%d" % rk[p]], len(serve(p)), plan["collect"][p]))
    for (s, p, b) in plan["relays"]:
        if b == me:
            arrivals.append((S["r%d" % rk[s]], len(_engines(topo.mask(p, core))), [s]))
    order = [s for (sem, cnt, owners) in arrivals for s in owners]

    h = slice(0, TK)
    pe.wait_ge(S.ldx, 32)
    pe.matmul(T.ps_s[h, 0:N], T.xs[:, :], T.rts[:, :], True, True).then_inc(S.p_s, 1)
    pe.wait_ge(S.idn, 1)
    pe.matmul(T.ps_t[h, 0:D], T.xs[:, :], T.ident[:, :], True, True).then_inc(S.p_t, 1)

    ve.wait_ge(S.p_s, 1)
    ve.tensor_reduce(T.nm[h, 0:1], T.ps_s[h, 0:N], AxisListType.X, AluOpType.max, negate=True).then_inc(S.v_nm, 1)
    ac.wait_ge(S.v_nm, 1)
    ac.activation(T.ex[h, 0:N], T.ps_s[h, 0:N], ActivationFunctionType.Exp, bias=T.nm[h, 0:1], scale=1.0,
                  accum_out=T.ssum[h, 0:1]).then_inc(S.a_e, 1)
    ac.wait_ge(S.a_e, 1)
    ac.wait_ge(S.idn, 1)
    for k in range(NA):
        j = rk[order[k]]
        ac.activation(T.dg[h, k * TK:(k + 1) * TK], T.ident[h, 0:TK], ActivationFunctionType.Copy,
                      scale=T.ex[h, j:j + 1]).then_inc(S.v_da, 1)
    ve.wait_ge(S.a_e, 1)
    ve.reciprocal(T.rs[h, 0:1], T.ssum[h, 0:1]).then_inc(S.v_rs, 1)
    ve.wait_ge(S.v_rs, 1)
    ve.wait_ge(S.p_t, 1)
    ve.tensor_scalar(T.xt[h, :], T.ps_t[h, 0:D], T.rs[h, 0:1], None, mult).then_inc(S.v_xt, 1)
    ve.wait_ge(S.idn, 1)
    for k in range(NA, N):
        j = rk[order[k]]
        ve.tensor_scalar(T.dg[h, k * TK:(k + 1) * TK], T.ident[h, 0:TK], T.ex[h, j:j + 1], None,
                         mult).then_inc(S.v_db, 1)
    pe.wait_ge(S.v_xt, 1)
    pe.wait_ge(S.v_da, NA)
    pe.matmul(T.ps_a[:, 0:NA * TK], T.xt[h, :], T.dg[h, 0:NA * TK], True, True).then_inc(S.p_a, 1)
    pe.wait_ge(S.v_db, N - NA)
    pe.matmul(T.ps_b[:, 0:(N - NA) * TK], T.xt[h, :], T.dg[h, NA * TK:N * TK], True, True).then_inc(S.p_b, 1)
    ve.wait_ge(S.p_a, 1)
    ve.tensor_copy(T.xg[:, 0:NA * TK], T.ps_a[:, 0:NA * TK]).then_inc(S.c_a, 1)
    ac.wait_ge(S.p_b, 1)
    ac.activation(T.xg[:, NA * TK:N * TK], T.ps_b[:, 0:(N - NA) * TK], ActivationFunctionType.Copy).then_inc(S.c_b, 1)

    k = 0
    pe.wait_ge(S.c_a, 1)
    for sem, cnt, owners in arrivals:
        pe.wait_ge(sem, cnt)
        for s in owners:
            if k == NA:
                pe.wait_ge(S.c_b, 1)
            mm = pe.matmul(T.ps_y[:, 0:TK], blocks(me, s), T.xg[:, k * TK:(k + 1) * TK], k == 0, k == N - 1)
            k += 1
    mm.then_inc(S.p_y, 1)

    ve.wait_ge(S.p_y, 1)
    ve.tensor_copy(T.ysb[:, :], T.ps_y[:, 0:TK]).then_inc(S.v_y, 1)
    sp.wait_ge(S.v_y, 1)
    sp.dma_start(T.y[:, :], T.ysb[:, :]).then_inc(S.st, 16)
    sp.wait_ge(S.st, 16)
